import numpy as np
import ml_dtypes


def mxq(x, axis, fmt="e4m3"):
    dtype, down = {"e4m3": (ml_dtypes.float8_e4m3fn, 7), "e5m2": (ml_dtypes.float8_e5m2, 14)}[fmt]
    v = np.moveaxis(np.asarray(x, np.float32).astype(ml_dtypes.bfloat16).astype(np.float64), axis, -1)
    blocks = v.reshape(v.shape[:-1] + (-1, 32))
    amax = np.abs(blocks).max(-1, keepdims=True)
    byte = np.maximum(np.where(amax > 0, np.frexp(amax)[1] - 1 + 127, 0) - down, 1)
    scale = np.exp2(byte - 127.0)
    codes = (blocks / scale).astype(np.float32).astype(dtype).astype(np.float64)
    return np.moveaxis((codes * scale).reshape(v.shape), -1, axis)


WIDE = False


def mx_kscale(k):
    if not WIDE:
        return np.ones(k)
    levels = np.array([10, -10, 5, -5, 0])
    if k % 512:
        return np.exp2(np.random.permutation(np.resize(levels, k // 32))).repeat(32)
    a = np.empty((k // 512, 16))
    for p in range(k // 512):
        a[p, :8] = np.random.permutation(np.resize(levels, 8))
        for g in range(8):
            far = levels[np.abs(levels - a[p, g]) >= 10]
            a[p, g + 8] = far[np.random.randint(len(far))]
    return np.exp2(a.ravel()).repeat(32)


def f64(x):
    return np.asarray(x).astype(np.float64)


def striped(idx):
    return np.tile(np.asarray(idx).reshape(-1, 16).T, (8, 1)).astype(np.uint16)


def unstriped(offs):
    return offs[:16].T.reshape(-1).astype(np.int64)


E2M1 = np.array([0.0, 0.5, 1.0, 1.5, 2.0, 3.0, 4.0, 6.0, -0.0, -0.5, -1.0, -1.5, -2.0, -3.0, -4.0, -6.0])


def pack_weight(w, fmt):
    k, n = w.shape
    w = f64(np.asarray(w, np.float32).astype(ml_dtypes.bfloat16)).reshape(k // 32, 32, n)
    amax = np.abs(w).max(1)
    if fmt == "e4m3":
        byte = np.frexp(amax)[1] - 1 + 127 - 7
    else:
        mant, ex = np.frexp(amax / 6.0)
        byte = np.where(mant > 0.5, ex, ex - 1) + 127
    byte = np.clip(np.where(amax > 0, byte, 1), 1, 254)
    scaled = (w * np.exp2(127.0 - byte)[:, None, :]).reshape(k, n).astype(np.float32)
    by_word = np.ascontiguousarray(scaled.reshape(k // 512, 128, 4, n).transpose(0, 1, 3, 2))
    if fmt == "e4m3":
        words = by_word.astype(ml_dtypes.float8_e4m3fn).view(np.uint8)
    else:
        c = by_word.astype(ml_dtypes.float4_e2m1fn).view(np.uint8) & 0xF
        words = (c[..., 0::2] | (c[..., 1::2] << 4)).reshape(k // 512, 128, 2 * n)
    return np.ascontiguousarray(words), np.ascontiguousarray(byte.astype(np.uint8).reshape(k // 512, 16, n))


def unpack_weight(words, scales, fmt):
    g, _, n = scales.shape
    words = np.ascontiguousarray(words).reshape(g, 128, n, -1)
    if fmt == "e4m3":
        vals = words.view(ml_dtypes.float8_e4m3fn).astype(np.float64)
    else:
        nib = np.empty((g, 128, n, 4), np.uint8)
        nib[..., 0::2] = words & 0xF
        nib[..., 1::2] = words >> 4
        vals = E2M1[nib]
    vals = vals * np.repeat(np.exp2(scales.astype(np.float64) - 127.0), 8, axis=1)[..., None]
    return vals.transpose(0, 1, 3, 2).reshape(g * 512, n)


D, E, T, I, Q = 512, 512, 2048, 512, 128


def setup_inputs():
    n = np.random.standard_normal
    idx = np.random.permutation(T)[:I]
    fd = mx_kscale(D)
    fe = mx_kscale(E)
    fi = mx_kscale(I)
    ti = np.ones(T)
    ti[idx] = fi
    keysp = pack_weight(n((D, T)) / fd[:, None], "e2m1")
    valsp = pack_weight(n((E, T)) / fe[:, None], "e2m1")
    return {
        "query": (n((D, Q)) * 0.6 / np.sqrt(D) * fd[:, None]).astype(np.float32),
        "keys_words": keysp[0],
        "keys_scales": keysp[1],
        "z0": (np.random.uniform(200.0, 800.0, (Q, 1))).astype(np.float32),
        "c00": (np.random.uniform(-100.0, 100.0, (Q, 1))).astype(np.float32),
        "disc": (np.random.uniform(0.3, 1.0, (Q, 1))).astype(np.float32),
        "size": (np.random.uniform(0.5, 2.0, (1, I))).astype(np.float32),
        "gout": (n((E, Q)) * 1 / np.sqrt(E) * fe[:, None]).astype(np.float32),
        "vals_words": valsp[0],
        "vals_scales": valsp[1],
        "fs": (np.random.uniform(128.0, 512.0, (1, I)) * fi).astype(np.float32),
        "keyrows": (n((D, T)) / ti).astype(np.float32),
        "res": (n((Q, D)) * 4.0).astype(np.float32),
        "offs": striped(idx),
    }


def reference(query, keys_words, keys_scales, z0, c00, disc, size, gout, vals_words, vals_scales, fs, keyrows, res, offs):
    idx = unstriped(offs)
    keysu = unpack_weight(keys_words, keys_scales, "e2m1")
    valsu = unpack_weight(vals_words, vals_scales, "e2m1")
    queryq = mxq(f64(query), 0, "e4m3")
    keysidxg = keysu[:, idx]
    a = queryq.T @ keysidxg
    p = np.exp(a)
    z = np.sum(p, axis=1, keepdims=True) + f64(z0) * f64(disc)
    goutq = mxq(f64(gout), 0, "e4m3")
    valsidxg = valsu[:, idx]
    c0 = goutq.T @ valsidxg
    dz = (np.sum(p * f64(size) * c0, axis=1, keepdims=True) + f64(c00) * f64(disc)) / np.square(z) * (-1.0)
    dp = 1.0 / z * c0 * f64(size) + dz
    da = dp * p
    gs = da * f64(fs)
    gt1 = gs.T
    kt = f64(keyrows)[:, idx].T
    gt1q = mxq(gt1, 0, "e4m3")
    ktq = mxq(kt, 0, "e4m3")
    gq = gt1q.T @ ktq
    y = gq + f64(res)
    return y

@@ -1,0 +1,198 @@
+from contextlib import ExitStack
+
+import concourse.mybir as mybir
+from concourse.masks import make_identity
+
+D, E, T, I, Q = 512, 512, 2048, 512, 128
+FLOPS = 2 * Q * I * (D + E + D)
+
+F32 = mybir.dt.float32
+BF16 = mybir.dt.bfloat16
+I32 = mybir.dt.int32
+U32 = mybir.dt.uint32
+U16 = mybir.dt.uint16
+U8 = mybir.dt.uint8
+FP8X4 = mybir.dt.float8_e4m3fn_x4
+FP4X4 = mybir.dt.float4_e2m1fn_x4
+ALU = mybir.AluOpType
+ACT = mybir.ActivationFunctionType
+
+P = 128
+PACK = 4
+
+
+def tile_attend_bresumed_q_kernel(tc, query, keys_words, keys_scales, z0, c00, disc, size, gout,
+                                   vals_words, vals_scales, fs, keyrows, res, offs, out):
+    nc = tc.nc
+    with ExitStack() as ctx:
+        held = ctx.enter_context(tc.tile_pool(name="held", bufs=1))
+        psum = ctx.enter_context(tc.psum_pool(name="psum", bufs=1))
+
+        def sb(name, shape, dtype, tag=None):
+            return held.tile(shape, dtype, name=name, tag=tag or name, align_bytes=64)
+
+        offsets = held.tile([P, I // 16], U16, name="offsets")
+        nc.sync.dma_start(offsets[:], offs)
+
+        ks_win = sb("ks_win", [P, T], U8)
+        vs_win = sb("vs_win", [P, T], U8, tag="slot1")
+        for win, src in ((ks_win, keys_scales), (vs_win, vals_scales)):
+            rows = src[0].bitcast(I32).unsqueeze(1).broadcast_to([16, 2, T // 4])
+            nc.sync.dma_start(win[96:P, :].bitcast(I32), rows)
+            nc.vector.memset(win[0:96, :].bitcast(I32), 0)
+
+        kw_win = sb("kw_win", [P, T], U16, tag="slot2")
+        vw_win = sb("vw_win", [P, T], U16, tag="slot3")
+        q_raw = sb("q_raw", [P, PACK, Q], F32)
+        g_raw = sb("g_raw", [P, PACK, Q], F32)
+        nc.sync.dma_start(kw_win[:].bitcast(I32), keys_words[0].bitcast(I32))
+        nc.sync.dma_start(q_raw[:], query.rearrange("(p j) w -> p j w", j=PACK))
+        nc.sync.dma_start(vw_win[:].bitcast(I32), vals_words[0].bitcast(I32))
+        nc.sync.dma_start(g_raw[:], gout.rearrange("(p j) w -> p j w", j=PACK))
+        kr_win = []
+
+        def load_plane(j):
+            kr_win.append(sb("kr_win%d" % j, [P, T], F32, tag="slot%d" % j))
+            nc.sync.dma_start(kr_win[j][:], keyrows[P * j : P * (j + 1), :])
+
+        load_plane(0)
+
+        size_col = sb("size_col", [P, PACK], F32)
+        fs_col = sb("fs_col", [P, PACK], F32)
+        z0_col = sb("z0_col", [P, 1], F32)
+        disc_col = sb("disc_col", [P, 1], F32)
+        c00_col = sb("c00_col", [P, 1], F32)
+        ident = sb("ident", [P, P], F32)
+        planes = sb("planes", [P, 2 * I], U8)
+        nc.scalar.dma_start(size_col[:], size.rearrange("o (p r) -> (o p) r", r=PACK))
+        nc.scalar.dma_start(fs_col[:], fs.rearrange("o (p r) -> (o p) r", r=PACK))
+        make_identity(nc, ident[:])
+        nc.vector.memset(planes[:].bitcast(I32), 0)
+        nc.gpsimd.dma_start(z0_col[:], z0)
+        nc.gpsimd.dma_start(disc_col[:], disc)
+        nc.gpsimd.dma_start(c00_col[:], c00)
+
+        warm = sb("warm", [P, 1], F32)
+        warm_out = sb("warm_out", [P, 1], F32)
+        nc.vector.memset(warm[:], 0.0)
+        nc.scalar.activation(warm_out[:], warm[:], ACT.Exp)
+
+        picked = sb("picked", [P, 2 * I], U8)
+        nc.vector.tensor_copy(picked[:, 0:I], ks_win[:].indirect(offsets[:]))
+        nc.vector.tensor_copy(picked[:, I : 2 * I], vs_win[:].indirect(offsets[:]))
+        for j in range(4):
+            nc.scalar.dma_start(planes[32 * j : 32 * j + 4, :].bitcast(I32), picked[96 + 8 * j : 96 + 8 * j + 8 : 2, :].bitcast(I32))
+        load_plane(1)
+
+        kw = sb("kw", [P, I], U16)
+        vw = sb("vw", [P, I], U16)
+        q_bf = sb("q_bf", [P, Q, PACK], BF16)
+        g_bf = sb("g_bf", [P, Q, PACK], BF16)
+        q_codes = sb("q_codes", [P, Q], U32)
+        g_codes = sb("g_codes", [P, Q], U32)
+        q_sc = sb("q_sc", [P, Q], U8)
+        g_sc = sb("g_sc", [P, Q], U8)
+
+        nc.scalar.copy(q_bf[:], q_raw[:].rearrange("p j w -> p w j"))
+        nc.vector.tensor_copy(kw[:], kw_win[:].indirect(offsets[:]))
+        load_plane(2)
+        nc.vector.quantize_mx(q_codes[:].bitcast(FP8X4), q_sc[:], q_bf[:].rearrange("p w j -> p (w j)"))
+        nc.scalar.copy(g_bf[:], g_raw[:].rearrange("p j w -> p w j"))
+        nc.vector.tensor_copy(vw[:], vw_win[:].indirect(offsets[:]))
+        load_plane(3)
+        nc.vector.quantize_mx(g_codes[:].bitcast(FP8X4), g_sc[:], g_bf[:].rearrange("p w j -> p (w j)"))
+
+        nfs_col = sb("nfs_col", [P, PACK], F32)
+        nc.gpsimd.tensor_scalar(nfs_col[:], fs_col[:], -1.0, 0.0, ALU.mult, ALU.add)
+        size_ps = psum.tile([P, PACK, P], F32, name="size_ps", tag="bank_sz")
+        nfs_ps = psum.tile([P, PACK, P], F32, name="nfs_ps", tag="bank_fs")
+        for r in range(PACK):
+            nc.tensor.transpose(size_ps[:, r, :], size_col[:, r : r + 1].to_broadcast([P, P]), ident[:])
+        for r in range(PACK):
+            nc.tensor.transpose(nfs_ps[:, r, :], nfs_col[:, r : r + 1].to_broadcast([P, P]), ident[:])
+        size_row = sb("size_row", [P, P, PACK], F32)
+        nc.scalar.copy(size_row[:], size_ps[:].rearrange("q r p -> q p r"))
+
+        zd = sb("zd", [P, 1], F32)
+        cd = sb("cd", [P, 1], F32)
+        nc.gpsimd.tensor_tensor(zd[:], z0_col[:], disc_col[:], ALU.mult)
+        nc.gpsimd.tensor_tensor(cd[:], c00_col[:], disc_col[:], ALU.mult)
+
+        a_ps = psum.tile([P, I], F32, name="a_ps", tag="bank_a")
+        c_ps = psum.tile([P, I], F32, name="c_ps", tag="bank_c")
+        nc.tensor.matmul_mx(a_ps[:], lhsT=q_codes[:].bitcast(FP8X4), lhsT_scale=q_sc[:],
+                            rhs=kw[:].bitcast(FP4X4), rhs_scale=planes[:, 0:I], start=True, stop=True)
+        nc.tensor.matmul_mx(c_ps[:], lhsT=g_codes[:].bitcast(FP8X4), lhsT_scale=g_sc[:],
+                            rhs=vw[:].bitcast(FP4X4), rhs_scale=planes[:, I : 2 * I], start=True, stop=True)
+
+        kt_codes = sb("kt_codes", [P, D], U32)
+        kt_sc = sb("kt_sc", [P, D], U8)
+
+        def turn(src_bf, bank, dst_bf):
+            words = src_bf.bitcast(F32)
+            for u in range(2):
+                nc.tensor.transpose(bank[:, u, :], words[:, u : 2 * P : 2], ident[:])
+            nc.scalar.copy(dst_bf.bitcast(F32).rearrange("p (x u) -> p x u", u=2), bank.rearrange("p u x -> p x u"))
+
+        kt_bf = [sb("kt_bf%d" % j, [P, P * PACK], BF16) for j in range(4)]
+
+        def gather_plane(j):
+            kr = sb("kr%d" % j, [P, I], BF16)
+            nc.vector.tensor_copy(kr[:], kr_win[j][:].indirect(offsets[:]))
+            bank = psum.tile([P, 2, P], F32, name="kt_ps%d" % j, tag="kt_ps%d" % j)
+            turn(kr[:], bank[:], kt_bf[j][:])
+
+        def quantize_plane(j):
+            cols = slice(P * j, P * (j + 1))
+            nc.vector.quantize_mx(kt_codes[:, cols].bitcast(FP8X4), kt_sc[:, cols], kt_bf[j][:])
+
+        gather_plane(0)
+        res_sb = sb("res_sb", [P, D], F32, tag="slot0")
+        nc.sync.dma_start(res_sb[:], res)
+
+        p_sb = sb("p_sb", [P, I], F32)
+        p_sum = sb("p_sum", [P, 1], F32)
+        nc.scalar.activation(p_sb[:], a_ps[:], ACT.Exp, accum_out=p_sum[:])
+        v_sb = sb("v_sb", [P, I], F32)
+        nc.vector.tensor_tensor(v_sb[:], c_ps[:], size_row[:].rearrange("q p r -> q (p r)"), ALU.mult)
+        z = sb("z", [P, 1], F32)
+        nc.vector.tensor_tensor(z[:], p_sum[:], zd[:], ALU.add)
+        t_sb = sb("t_sb", [P, I], F32)
+        t_sum = sb("t_sum", [P, 1], F32)
+        nc.vector.scalar_tensor_tensor(t_sb[:], v_sb[:], 1.0, p_sb[:], ALU.mult, ALU.mult, accum_out=t_sum[:])
+        rz = sb("rz", [P, 1], F32)
+        nc.vector.reciprocal(rz[:], z[:])
+        w = sb("w", [P, 1], F32)
+        nc.vector.tensor_scalar(w[:], t_sum[:], cd[:], rz[:], ALU.add, ALU.mult)
+        quantize_plane(0)
+        y_sb = sb("y_sb", [P, I], F32)
+        nc.vector.scalar_tensor_tensor(y_sb[:], p_sb[:], w[:], t_sb[:], ALU.mult, ALU.subtract)
+        gs = sb("gs", [P, I], BF16)
+        nc.vector.scalar_tensor_tensor(gs[:].rearrange("q (p r) -> q p r", r=PACK),
+                                       y_sb[:].rearrange("q (p r) -> q p r", r=PACK), rz[:],
+                                       nfs_ps[:].rearrange("q r p -> q p r"), ALU.mult, ALU.mult)
+        gt_ps = psum.tile([P, 2, P], F32, name="gt_ps", tag="bank_sz")
+        gt_bf = sb("gt_bf", [P, Q * PACK], BF16)
+        turn(gs[:], gt_ps[:], gt_bf[:])
+        gather_plane(1)
+        gt_codes = sb("gt_codes", [P, Q], U32)
+        gt_sc = sb("gt_sc", [P, Q], U8)
+        nc.vector.quantize_mx(gt_codes[:].bitcast(FP8X4), gt_sc[:], gt_bf[:])
+        gather_plane(2)
+        quantize_plane(1)
+        gather_plane(3)
+        quantize_plane(2)
+
+        def finish(lo, hi, tag):
+            acc = psum.tile([P, hi - lo], F32, name="acc%d" % lo, tag=tag)
+            nc.tensor.matmul_mx(acc[:], lhsT=gt_codes[:].bitcast(FP8X4), lhsT_scale=gt_sc[:],
+                                rhs=kt_codes[:, lo:hi].bitcast(FP8X4), rhs_scale=kt_sc[:, lo:hi],
+                                start=True, stop=True)
+            y = sb("y%d" % lo, [P, hi - lo], F32)
+            nc.vector.tensor_tensor(y[:], acc[:], res_sb[:, lo:hi], ALU.add)
+            nc.sync.dma_start(out[:, lo:hi], y[:])
+
+        finish(0, 2 * P, "bank_a")
+        finish(2 * P, 3 * P, "bank_c")
+        quantize_plane(3)
+        finish(3 * P, 4 * P, "bank_fs")

@@ -1,7 +1,6 @@
 from contextlib import ExitStack
 
 import concourse.mybir as mybir
-from concourse.masks import make_identity
 
 D, E, T, I, Q = 512, 512, 2048, 512, 128
 FLOPS = 2 * Q * I * (D + E + D)
@@ -26,6 +25,7 @@ def tile_attend_bresumed_q_kernel(tc, query, keys_words, keys_scales, z0, c00, d
     nc = tc.nc
     with ExitStack() as ctx:
         held = ctx.enter_context(tc.tile_pool(name="held", bufs=1))
+        early = ctx.enter_context(tc.tile_pool(name="early", bufs=1))
         psum = ctx.enter_context(tc.psum_pool(name="psum", bufs=1))
 
         def sb(name, shape, dtype, tag=None):
@@ -34,18 +34,33 @@ def tile_attend_bresumed_q_kernel(tc, query, keys_words, keys_scales, z0, c00, d
         offsets = held.tile([P, I // 16], U16, name="offsets")
         nc.sync.dma_start(offsets[:], offs)
 
+        ident = sb("ident", [P, P], F32)
+        ones = early.tile([P, P], F32, name="ones", offset=0)
+        col_no = sb("col_no", [P, P], F32)
+        row_no = sb("row_no", [P, 32], F32)
+        nc.vector.memset(ones[:], 1.0)
+        nc.vector.tensor_tensor_scan(col_no[:], ones[:], ones[:], 0.0, ALU.mult, ALU.add)
+        nc.vector.transpose(row_no[:], col_no[:, 0:32])
+        for a in range(4):
+            quad = slice(32 * a, 32 * (a + 1))
+            nc.vector.tensor_scalar(ident[quad, :], col_no[quad, :], -32.0 * a, row_no[quad, 0:1], ALU.add, ALU.is_equal)
+
         ks_win = sb("ks_win", [P, T], U8)
-        vs_win = sb("vs_win", [P, T], U8, tag="slot1")
+        vs_win = sb("vs_win", [P, T], U8)
         for win, src in ((ks_win, keys_scales), (vs_win, vals_scales)):
             rows = src[0].bitcast(I32).unsqueeze(1).broadcast_to([16, 2, T // 4])
             nc.sync.dma_start(win[96:P, :].bitcast(I32), rows)
-            nc.vector.memset(win[0:96, :].bitcast(I32), 0)
+            nc.gpsimd.memset(win[0:96, :].bitcast(I32), 0)
 
-        kw_win = sb("kw_win", [P, T], U16, tag="slot2")
-        vw_win = sb("vw_win", [P, T], U16, tag="slot3")
-        q_raw = sb("q_raw", [P, PACK, Q], F32)
-        g_raw = sb("g_raw", [P, PACK, Q], F32)
+        kw_win = sb("kw_win", [P, T], U16)
+        vw_win = sb("vw_win", [P, T], U16)
+        q_raw = sb("q_raw", [P, PACK, Q], F32, tag="slot1")
+        g_raw = sb("g_raw", [P, PACK, Q], F32, tag="slot2")
         nc.sync.dma_start(kw_win[:].bitcast(I32), keys_words[0].bitcast(I32))
+        size_col = sb("size_col", [P, PACK], F32)
+        fs_col = sb("fs_col", [P, PACK], F32)
+        nc.sync.dma_start(size_col[:], size.rearrange("o (p r) -> (o p) r", r=PACK))
+        nc.sync.dma_start(fs_col[:], fs.rearrange("o (p r) -> (o p) r", r=PACK))
         nc.sync.dma_start(q_raw[:], query.rearrange("(p j) w -> p j w", j=PACK))
         nc.sync.dma_start(vw_win[:].bitcast(I32), vals_words[0].bitcast(I32))
         nc.sync.dma_start(g_raw[:], gout.rearrange("(p j) w -> p j w", j=PACK))
@@ -57,76 +72,54 @@ def tile_attend_bresumed_q_kernel(tc, query, keys_words, keys_scales, z0, c00, d
 
         load_plane(0)
 
-        size_col = sb("size_col", [P, PACK], F32)
-        fs_col = sb("fs_col", [P, PACK], F32)
-        z0_col = sb("z0_col", [P, 1], F32)
-        disc_col = sb("disc_col", [P, 1], F32)
-        c00_col = sb("c00_col", [P, 1], F32)
-        ident = sb("ident", [P, P], F32)
+        z0_col = early.tile([P, 1], F32, name="z0_col", offset=0)
+        disc_col = early.tile([P, 1], F32, name="disc_col", offset=64)
+        c00_col = early.tile([P, 1], F32, name="c00_col", offset=128)
         planes = sb("planes", [P, 2 * I], U8)
-        nc.scalar.dma_start(size_col[:], size.rearrange("o (p r) -> (o p) r", r=PACK))
-        nc.scalar.dma_start(fs_col[:], fs.rearrange("o (p r) -> (o p) r", r=PACK))
-        make_identity(nc, ident[:])
         nc.vector.memset(planes[:].bitcast(I32), 0)
         nc.gpsimd.dma_start(z0_col[:], z0)
         nc.gpsimd.dma_start(disc_col[:], disc)
         nc.gpsimd.dma_start(c00_col[:], c00)
 
-        warm = sb("warm", [P, 1], F32)
         warm_out = sb("warm_out", [P, 1], F32)
-        nc.vector.memset(warm[:], 0.0)
-        nc.scalar.activation(warm_out[:], warm[:], ACT.Exp)
+        nc.scalar.activation(warm_out[:], col_no[:, 0:1], ACT.Exp)
 
-        picked = sb("picked", [P, 2 * I], U8)
-        nc.vector.tensor_copy(picked[:, 0:I], ks_win[:].indirect(offsets[:]))
-        nc.vector.tensor_copy(picked[:, I : 2 * I], vs_win[:].indirect(offsets[:]))
-        for j in range(4):
-            nc.scalar.dma_start(planes[32 * j : 32 * j + 4, :].bitcast(I32), picked[96 + 8 * j : 96 + 8 * j + 8 : 2, :].bitcast(I32))
-        load_plane(1)
-
-        kw = sb("kw", [P, I], U16)
-        vw = sb("vw", [P, I], U16)
-        q_bf = sb("q_bf", [P, Q, PACK], BF16)
-        g_bf = sb("g_bf", [P, Q, PACK], BF16)
-        q_codes = sb("q_codes", [P, Q], U32)
-        g_codes = sb("g_codes", [P, Q], U32)
-        q_sc = sb("q_sc", [P, Q], U8)
-        g_sc = sb("g_sc", [P, Q], U8)
-
-        nc.scalar.copy(q_bf[:], q_raw[:].rearrange("p j w -> p w j"))
-        nc.vector.tensor_copy(kw[:], kw_win[:].indirect(offsets[:]))
-        load_plane(2)
-        nc.vector.quantize_mx(q_codes[:].bitcast(FP8X4), q_sc[:], q_bf[:].rearrange("p w j -> p (w j)"))
-        nc.scalar.copy(g_bf[:], g_raw[:].rearrange("p j w -> p w j"))
-        nc.vector.tensor_copy(vw[:], vw_win[:].indirect(offsets[:]))
-        load_plane(3)
-        nc.vector.quantize_mx(g_codes[:].bitcast(FP8X4), g_sc[:], g_bf[:].rearrange("p w j -> p (w j)"))
-
-        nfs_col = sb("nfs_col", [P, PACK], F32)
-        nc.gpsimd.tensor_scalar(nfs_col[:], fs_col[:], -1.0, 0.0, ALU.mult, ALU.add)
         size_ps = psum.tile([P, PACK, P], F32, name="size_ps", tag="bank_sz")
         nfs_ps = psum.tile([P, PACK, P], F32, name="nfs_ps", tag="bank_fs")
         for r in range(PACK):
             nc.tensor.transpose(size_ps[:, r, :], size_col[:, r : r + 1].to_broadcast([P, P]), ident[:])
         for r in range(PACK):
-            nc.tensor.transpose(nfs_ps[:, r, :], nfs_col[:, r : r + 1].to_broadcast([P, P]), ident[:])
+            nc.tensor.transpose(nfs_ps[:, r, :], fs_col[:, r : r + 1].to_broadcast([P, P]), ident[:])
         size_row = sb("size_row", [P, P, PACK], F32)
         nc.scalar.copy(size_row[:], size_ps[:].rearrange("q r p -> q p r"))
 
-        zd = sb("zd", [P, 1], F32)
-        cd = sb("cd", [P, 1], F32)
-        nc.gpsimd.tensor_tensor(zd[:], z0_col[:], disc_col[:], ALU.mult)
-        nc.gpsimd.tensor_tensor(cd[:], c00_col[:], disc_col[:], ALU.mult)
+        picked = sb("picked", [P, 2 * I], U8)
+        nc.vector.tensor_copy(picked[:, 0:I], ks_win[:].indirect(offsets[:]))
+        nc.vector.tensor_copy(picked[:, I : 2 * I], vs_win[:].indirect(offsets[:]))
+        for j in range(4):
+            nc.sync.dma_start(planes[32 * j : 32 * j + 4, :].bitcast(I32), picked[96 + 8 * j : 96 + 8 * j + 8 : 2, :].bitcast(I32))
+
+        kw = sb("kw", [P, I], U16)
+        vw = sb("vw", [P, I], U16)
+        qg_bf = sb("qg_bf", [P, 2, Q, PACK], BF16, tag="slot3")
+        qg_codes = sb("qg_codes", [P, 2 * Q], U32, tag="fs_col")
+        qg_sc = sb("qg_sc", [P, 2 * Q], U8)
+
+        nc.scalar.copy(qg_bf[:, 0], q_raw[:].rearrange("p j w -> p w j"))
+        load_plane(1)
+        nc.vector.tensor_copy(kw[:], kw_win[:].indirect(offsets[:]))
+        nc.scalar.copy(qg_bf[:, 1], g_raw[:].rearrange("p j w -> p w j"))
+        load_plane(2)
+        nc.vector.tensor_copy(vw[:], vw_win[:].indirect(offsets[:]))
+        nc.vector.quantize_mx(qg_codes[:].bitcast(FP8X4), qg_sc[:], qg_bf[:].rearrange("p s w j -> p (s w j)"))
+        load_plane(3)
 
         a_ps = psum.tile([P, I], F32, name="a_ps", tag="bank_a")
         c_ps = psum.tile([P, I], F32, name="c_ps", tag="bank_c")
-        nc.tensor.matmul_mx(a_ps[:], lhsT=q_codes[:].bitcast(FP8X4), lhsT_scale=q_sc[:],
+        nc.tensor.matmul_mx(a_ps[:], lhsT=qg_codes[:, 0:Q].bitcast(FP8X4), lhsT_scale=qg_sc[:, 0:Q],
                             rhs=kw[:].bitcast(FP4X4), rhs_scale=planes[:, 0:I], start=True, stop=True)
-        nc.tensor.matmul_mx(c_ps[:], lhsT=g_codes[:].bitcast(FP8X4), lhsT_scale=g_sc[:],
+        nc.tensor.matmul_mx(c_ps[:], lhsT=qg_codes[:, Q : 2 * Q].bitcast(FP8X4), lhsT_scale=qg_sc[:, Q : 2 * Q],
                             rhs=vw[:].bitcast(FP4X4), rhs_scale=planes[:, I : 2 * I], start=True, stop=True)
-
-        kt_codes = sb("kt_codes", [P, D], U32)
-        kt_sc = sb("kt_sc", [P, D], U8)
 
         def turn(src_bf, bank, dst_bf):
             words = src_bf.bitcast(F32)
@@ -134,29 +127,30 @@ def tile_attend_bresumed_q_kernel(tc, query, keys_words, keys_scales, z0, c00, d
                 nc.tensor.transpose(bank[:, u, :], words[:, u : 2 * P : 2], ident[:])
             nc.scalar.copy(dst_bf.bitcast(F32).rearrange("p (x u) -> p x u", u=2), bank.rearrange("p u x -> p x u"))
 
-        kt_bf = [sb("kt_bf%d" % j, [P, P * PACK], BF16) for j in range(4)]
+        kt_bf = sb("kt_bf", [P, D * PACK], BF16)
 
-        def gather_plane(j):
-            kr = sb("kr%d" % j, [P, I], BF16)
+        def turn_plane(j, kr):
+            bank = psum.tile([P, 2, P], F32, name="kt_ps%d" % j, tag="kt_ps%d" % j if j else "bank_a")
+            turn(kr[:], bank[:], kt_bf[:, I * j : I * (j + 1)])
+
+        def gather_plane(j, tag):
+            kr = sb("kr%d" % j, [P, I], BF16, tag=tag)
             nc.vector.tensor_copy(kr[:], kr_win[j][:].indirect(offsets[:]))
-            bank = psum.tile([P, 2, P], F32, name="kt_ps%d" % j, tag="kt_ps%d" % j)
-            turn(kr[:], bank[:], kt_bf[j][:])
+            turn_plane(j, kr)
 
-        def quantize_plane(j):
-            cols = slice(P * j, P * (j + 1))
-            nc.vector.quantize_mx(kt_codes[:, cols].bitcast(FP8X4), kt_sc[:, cols], kt_bf[j][:])
-
-        gather_plane(0)
-        res_sb = sb("res_sb", [P, D], F32, tag="slot0")
+        res_sb = sb("res_sb", [P, D], F32, tag="kw")
         nc.sync.dma_start(res_sb[:], res)
+        gather_plane(0, "kr0")
 
         p_sb = sb("p_sb", [P, I], F32)
         p_sum = sb("p_sum", [P, 1], F32)
         nc.scalar.activation(p_sb[:], a_ps[:], ACT.Exp, accum_out=p_sum[:])
-        v_sb = sb("v_sb", [P, I], F32)
-        nc.vector.tensor_tensor(v_sb[:], c_ps[:], size_row[:].rearrange("q p r -> q (p r)"), ALU.mult)
         z = sb("z", [P, 1], F32)
-        nc.vector.tensor_tensor(z[:], p_sum[:], zd[:], ALU.add)
+        nc.scalar.activation(z[:], z0_col[:], ACT.Identity, bias=p_sum[:], scale=disc_col[:])
+        cd = early.tile([P, 1], F32, name="cd", offset=0)
+        nc.scalar.activation(cd[:], c00_col[:], ACT.Copy, scale=disc_col[:])
+        v_sb = sb("v_sb", [P, I], F32, tag="slot0")
+        nc.vector.tensor_tensor(v_sb[:], c_ps[:], size_row[:].rearrange("q p r -> q (p r)"), ALU.mult)
         t_sb = sb("t_sb", [P, I], F32)
         t_sum = sb("t_sum", [P, 1], F32)
         nc.vector.scalar_tensor_tensor(t_sb[:], v_sb[:], 1.0, p_sb[:], ALU.mult, ALU.mult, accum_out=t_sum[:])
@@ -164,35 +158,48 @@ def tile_attend_bresumed_q_kernel(tc, query, keys_words, keys_scales, z0, c00, d
         nc.vector.reciprocal(rz[:], z[:])
         w = sb("w", [P, 1], F32)
         nc.vector.tensor_scalar(w[:], t_sum[:], cd[:], rz[:], ALU.add, ALU.mult)
-        quantize_plane(0)
         y_sb = sb("y_sb", [P, I], F32)
         nc.vector.scalar_tensor_tensor(y_sb[:], p_sb[:], w[:], t_sb[:], ALU.mult, ALU.subtract)
         gs = sb("gs", [P, I], BF16)
         nc.vector.scalar_tensor_tensor(gs[:].rearrange("q (p r) -> q p r", r=PACK),
                                        y_sb[:].rearrange("q (p r) -> q p r", r=PACK), rz[:],
                                        nfs_ps[:].rearrange("q r p -> q p r"), ALU.mult, ALU.mult)
+        kr1_bf = sb("kr1_bf", [P, T], BF16)
+        for h in range(2):
+            half = slice(h * T // 2, (h + 1) * T // 2)
+            nc.scalar.activation(kr1_bf[:, half], kr_win[1][:, half], ACT.Copy)
+        kr1 = sb("kr1", [P, I], BF16)
+        nc.scalar.activation(kr1[:], kr1_bf[:].indirect(offsets[:]), ACT.Copy)
+
         gt_ps = psum.tile([P, 2, P], F32, name="gt_ps", tag="bank_sz")
-        gt_bf = sb("gt_bf", [P, Q * PACK], BF16)
+        gt_bf = sb("gt_bf", [P, Q * PACK], BF16, tag="kr1_bf")
         turn(gs[:], gt_ps[:], gt_bf[:])
-        gather_plane(1)
+
+        gather_plane(2, "y_sb")
+        turn_plane(1, kr1)
         gt_codes = sb("gt_codes", [P, Q], U32)
         gt_sc = sb("gt_sc", [P, Q], U8)
         nc.vector.quantize_mx(gt_codes[:].bitcast(FP8X4), gt_sc[:], gt_bf[:])
-        gather_plane(2)
-        quantize_plane(1)
-        gather_plane(3)
-        quantize_plane(2)
+        gather_plane(3, "t_sb")
 
-        def finish(lo, hi, tag):
-            acc = psum.tile([P, hi - lo], F32, name="acc%d" % lo, tag=tag)
-            nc.tensor.matmul_mx(acc[:], lhsT=gt_codes[:].bitcast(FP8X4), lhsT_scale=gt_sc[:],
+        kt_codes = sb("kt_codes", [P, D], U32, tag="slot3")
+        kt_sc = sb("kt_sc", [P, D], U8)
+
+        def multiply(lo, hi, acc):
+            nc.vector.quantize_mx(kt_codes[:, lo:hi].bitcast(FP8X4), kt_sc[:, lo:hi], kt_bf[:, PACK * lo : PACK * hi])
+            nc.tensor.matmul_mx(acc, lhsT=gt_codes[:].bitcast(FP8X4), lhsT_scale=gt_sc[:],
                                 rhs=kt_codes[:, lo:hi].bitcast(FP8X4), rhs_scale=kt_sc[:, lo:hi],
                                 start=True, stop=True)
-            y = sb("y%d" % lo, [P, hi - lo], F32)
-            nc.vector.tensor_tensor(y[:], acc[:], res_sb[:, lo:hi], ALU.add)
+
+        def finish(lo, hi, acc, tag):
+            y = sb("y%d" % lo, [P, hi - lo], F32, tag=tag)
+            nc.vector.tensor_tensor(y[:], res_sb[:, lo:hi], acc, ALU.subtract)
             nc.sync.dma_start(out[:, lo:hi], y[:])
 
-        finish(0, 2 * P, "bank_a")
-        finish(2 * P, 3 * P, "bank_c")
-        quantize_plane(3)
-        finish(3 * P, 4 * P, "bank_fs")
+        acc_a = psum.tile([P, 3 * P], F32, name="acc_a", tag="bank_a")
+        acc_b = psum.tile([P, P], F32, name="acc_b", tag="bank_c")
+        multiply(0, 2 * P, acc_a[:, 0 : 2 * P])
+        multiply(2 * P, 3 * P, acc_a[:, 2 * P : 3 * P])
+        multiply(3 * P, 4 * P, acc_b[:])
+        finish(0, 3 * P, acc_a[:], "kt_bf")
+        finish(3 * P, 4 * P, acc_b[:], "y_last")

@@ -18,6 +18,10 @@ ACT = mybir.ActivationFunctionType
 
 P = 128
 PACK = 4
+QUAD = 32
+QUADS = P // QUAD
+SCALE_ROWS = 16
+LAST_QUAD = P - QUAD
 
 
 def tile_attend_bresumed_q_kernel(tc, query, keys_words, keys_scales, z0, c00, disc, size, gout,
@@ -37,20 +41,21 @@ def tile_attend_bresumed_q_kernel(tc, query, keys_words, keys_scales, z0, c00, d
         ident = sb("ident", [P, P], F32)
         ones = early.tile([P, P], F32, name="ones", offset=0)
         col_no = sb("col_no", [P, P], F32)
-        row_no = sb("row_no", [P, 32], F32)
+        row_no = sb("row_no", [P, QUAD], F32)
         nc.vector.memset(ones[:], 1.0)
         nc.vector.tensor_tensor_scan(col_no[:], ones[:], ones[:], 0.0, ALU.mult, ALU.add)
-        nc.vector.transpose(row_no[:], col_no[:, 0:32])
-        for a in range(4):
-            quad = slice(32 * a, 32 * (a + 1))
-            nc.vector.tensor_scalar(ident[quad, :], col_no[quad, :], -32.0 * a, row_no[quad, 0:1], ALU.add, ALU.is_equal)
+        nc.vector.transpose(row_no[:], col_no[:, 0:QUAD])
+        for a in range(QUADS):
+            quad = slice(QUAD * a, QUAD * (a + 1))
+            nc.vector.tensor_scalar(ident[quad, :], col_no[quad, :], -float(QUAD * a), row_no[quad, 0:1],
+                                    ALU.add, ALU.is_equal)
 
         ks_win = sb("ks_win", [P, T], U8)
         vs_win = sb("vs_win", [P, T], U8)
         for win, src in ((ks_win, keys_scales), (vs_win, vals_scales)):
-            rows = src[0].bitcast(I32).unsqueeze(1).broadcast_to([16, 2, T // 4])
-            nc.sync.dma_start(win[96:P, :].bitcast(I32), rows)
-            nc.gpsimd.memset(win[0:96, :].bitcast(I32), 0)
+            rows = src[0].bitcast(I32).unsqueeze(1).broadcast_to([SCALE_ROWS, QUAD // SCALE_ROWS, T // 4])
+            nc.sync.dma_start(win[LAST_QUAD:P, :].bitcast(I32), rows)
+            nc.gpsimd.memset(win[0:LAST_QUAD, :].bitcast(I32), 0)
 
         kw_win = sb("kw_win", [P, T], U16)
         vw_win = sb("vw_win", [P, T], U16)
@@ -61,65 +66,64 @@ def tile_attend_bresumed_q_kernel(tc, query, keys_words, keys_scales, z0, c00, d
         fs_col = sb("fs_col", [P, PACK], F32)
         nc.sync.dma_start(size_col[:], size.rearrange("o (p r) -> (o p) r", r=PACK))
         nc.sync.dma_start(fs_col[:], fs.rearrange("o (p r) -> (o p) r", r=PACK))
-        nc.sync.dma_start(q_raw[:], query.rearrange("(p j) w -> p j w", j=PACK))
+        nc.sync.dma_start(q_raw[:], query.rearrange("(p r) q -> p r q", r=PACK))
         nc.sync.dma_start(vw_win[:].bitcast(I32), vals_words[0].bitcast(I32))
-        nc.sync.dma_start(g_raw[:], gout.rearrange("(p j) w -> p j w", j=PACK))
+        nc.sync.dma_start(g_raw[:], gout.rearrange("(p r) q -> p r q", r=PACK))
+
         kr_win = []
 
-        def load_plane(j):
+        def load_window(j):
             kr_win.append(sb("kr_win%d" % j, [P, T], F32, tag="slot%d" % j))
             nc.sync.dma_start(kr_win[j][:], keyrows[P * j : P * (j + 1), :])
 
-        load_plane(0)
+        load_window(0)
 
         z0_col = early.tile([P, 1], F32, name="z0_col", offset=0)
         disc_col = early.tile([P, 1], F32, name="disc_col", offset=64)
         c00_col = early.tile([P, 1], F32, name="c00_col", offset=128)
-        planes = sb("planes", [P, 2 * I], U8)
-        nc.vector.memset(planes[:].bitcast(I32), 0)
+        kv_scales = sb("kv_scales", [P, 2 * I], U8)
+        nc.vector.memset(kv_scales[:].bitcast(I32), 0)
         nc.gpsimd.dma_start(z0_col[:], z0)
         nc.gpsimd.dma_start(disc_col[:], disc)
         nc.gpsimd.dma_start(c00_col[:], c00)
 
-        warm_out = sb("warm_out", [P, 1], F32)
-        nc.scalar.activation(warm_out[:], col_no[:, 0:1], ACT.Exp)
-
-        size_ps = psum.tile([P, PACK, P], F32, name="size_ps", tag="bank_sz")
-        nfs_ps = psum.tile([P, PACK, P], F32, name="nfs_ps", tag="bank_fs")
+        size_ps = psum.tile([P, PACK, P], F32, name="size_ps", tag="bank_size")
+        fs_ps = psum.tile([P, PACK, P], F32, name="fs_ps", tag="bank_fs")
         for r in range(PACK):
             nc.tensor.transpose(size_ps[:, r, :], size_col[:, r : r + 1].to_broadcast([P, P]), ident[:])
         for r in range(PACK):
-            nc.tensor.transpose(nfs_ps[:, r, :], fs_col[:, r : r + 1].to_broadcast([P, P]), ident[:])
+            nc.tensor.transpose(fs_ps[:, r, :], fs_col[:, r : r + 1].to_broadcast([P, P]), ident[:])
         size_row = sb("size_row", [P, P, PACK], F32)
         nc.scalar.copy(size_row[:], size_ps[:].rearrange("q r p -> q p r"))
 
         picked = sb("picked", [P, 2 * I], U8)
         nc.vector.tensor_copy(picked[:, 0:I], ks_win[:].indirect(offsets[:]))
         nc.vector.tensor_copy(picked[:, I : 2 * I], vs_win[:].indirect(offsets[:]))
-        for j in range(4):
-            nc.sync.dma_start(planes[32 * j : 32 * j + 4, :].bitcast(I32), picked[96 + 8 * j : 96 + 8 * j + 8 : 2, :].bitcast(I32))
+        for a in range(QUADS):
+            first = LAST_QUAD + 2 * 4 * a
+            nc.sync.dma_start(kv_scales[QUAD * a : QUAD * a + 4, :].bitcast(I32),
+                              picked[first : first + 2 * 4 : 2, :].bitcast(I32))
 
         kw = sb("kw", [P, I], U16)
         vw = sb("vw", [P, I], U16)
         qg_bf = sb("qg_bf", [P, 2, Q, PACK], BF16, tag="slot3")
         qg_codes = sb("qg_codes", [P, 2 * Q], U32, tag="fs_col")
-        qg_sc = sb("qg_sc", [P, 2 * Q], U8)
-
-        nc.scalar.copy(qg_bf[:, 0], q_raw[:].rearrange("p j w -> p w j"))
-        load_plane(1)
+        qg_scales = sb("qg_scales", [P, 2 * Q], U8)
+        nc.scalar.activation(qg_bf[:, 0], q_raw[:].rearrange("p r q -> p q r"), ACT.Copy)
+        load_window(1)
         nc.vector.tensor_copy(kw[:], kw_win[:].indirect(offsets[:]))
-        nc.scalar.copy(qg_bf[:, 1], g_raw[:].rearrange("p j w -> p w j"))
-        load_plane(2)
+        nc.scalar.copy(qg_bf[:, 1], g_raw[:].rearrange("p r q -> p q r"))
+        load_window(2)
         nc.vector.tensor_copy(vw[:], vw_win[:].indirect(offsets[:]))
-        nc.vector.quantize_mx(qg_codes[:].bitcast(FP8X4), qg_sc[:], qg_bf[:].rearrange("p s w j -> p (s w j)"))
-        load_plane(3)
+        nc.vector.quantize_mx(qg_codes[:].bitcast(FP8X4), qg_scales[:], qg_bf[:].rearrange("p s q r -> p (s q r)"))
+        load_window(3)
 
         a_ps = psum.tile([P, I], F32, name="a_ps", tag="bank_a")
         c_ps = psum.tile([P, I], F32, name="c_ps", tag="bank_c")
-        nc.tensor.matmul_mx(a_ps[:], lhsT=qg_codes[:, 0:Q].bitcast(FP8X4), lhsT_scale=qg_sc[:, 0:Q],
-                            rhs=kw[:].bitcast(FP4X4), rhs_scale=planes[:, 0:I], start=True, stop=True)
-        nc.tensor.matmul_mx(c_ps[:], lhsT=qg_codes[:, Q : 2 * Q].bitcast(FP8X4), lhsT_scale=qg_sc[:, Q : 2 * Q],
-                            rhs=vw[:].bitcast(FP4X4), rhs_scale=planes[:, I : 2 * I], start=True, stop=True)
+        nc.tensor.matmul_mx(a_ps[:], lhsT=qg_codes[:, 0:Q].bitcast(FP8X4), lhsT_scale=qg_scales[:, 0:Q],
+                            rhs=kw[:].bitcast(FP4X4), rhs_scale=kv_scales[:, 0:I], start=True, stop=True)
+        nc.tensor.matmul_mx(c_ps[:], lhsT=qg_codes[:, Q : 2 * Q].bitcast(FP8X4), lhsT_scale=qg_scales[:, Q : 2 * Q],
+                            rhs=vw[:].bitcast(FP4X4), rhs_scale=kv_scales[:, I : 2 * I], start=True, stop=True)
 
         def turn(src_bf, bank, dst_bf):
             words = src_bf.bitcast(F32)
@@ -129,18 +133,18 @@ def tile_attend_bresumed_q_kernel(tc, query, keys_words, keys_scales, z0, c00, d
 
         kt_bf = sb("kt_bf", [P, D * PACK], BF16)
 
-        def turn_plane(j, kr):
-            bank = psum.tile([P, 2, P], F32, name="kt_ps%d" % j, tag="kt_ps%d" % j if j else "bank_a")
-            turn(kr[:], bank[:], kt_bf[:, I * j : I * (j + 1)])
+        def turn_window(j, kr, bank_tag):
+            bank = psum.tile([P, 2, P], F32, name="kt_ps%d" % j, tag=bank_tag)
+            turn(kr[:], bank[:], kt_bf[:, P * PACK * j : P * PACK * (j + 1)])
 
-        def gather_plane(j, tag):
+        def gather_window(j, tag, bank_tag):
             kr = sb("kr%d" % j, [P, I], BF16, tag=tag)
             nc.vector.tensor_copy(kr[:], kr_win[j][:].indirect(offsets[:]))
-            turn_plane(j, kr)
+            turn_window(j, kr, bank_tag)
 
         res_sb = sb("res_sb", [P, D], F32, tag="kw")
         nc.sync.dma_start(res_sb[:], res)
-        gather_plane(0, "kr0")
+        gather_window(0, "kr0", "bank_a")
 
         p_sb = sb("p_sb", [P, I], F32)
         p_sum = sb("p_sum", [P, 1], F32)
@@ -149,6 +153,7 @@ def tile_attend_bresumed_q_kernel(tc, query, keys_words, keys_scales, z0, c00, d
         nc.scalar.activation(z[:], z0_col[:], ACT.Identity, bias=p_sum[:], scale=disc_col[:])
         cd = early.tile([P, 1], F32, name="cd", offset=0)
         nc.scalar.activation(cd[:], c00_col[:], ACT.Copy, scale=disc_col[:])
+
         v_sb = sb("v_sb", [P, I], F32, tag="slot0")
         nc.vector.tensor_tensor(v_sb[:], c_ps[:], size_row[:].rearrange("q p r -> q (p r)"), ALU.mult)
         t_sb = sb("t_sb", [P, I], F32)
@@ -160,10 +165,12 @@ def tile_attend_bresumed_q_kernel(tc, query, keys_words, keys_scales, z0, c00, d
         nc.vector.tensor_scalar(w[:], t_sum[:], cd[:], rz[:], ALU.add, ALU.mult)
         y_sb = sb("y_sb", [P, I], F32)
         nc.vector.scalar_tensor_tensor(y_sb[:], p_sb[:], w[:], t_sb[:], ALU.mult, ALU.subtract)
-        gs = sb("gs", [P, I], BF16)
-        nc.vector.scalar_tensor_tensor(gs[:].rearrange("q (p r) -> q p r", r=PACK),
+        gather_window(2, "t_sb", "kt_ps2")
+        neg_gs = sb("neg_gs", [P, I], BF16, tag="slot2")
+        nc.vector.scalar_tensor_tensor(neg_gs[:].rearrange("q (p r) -> q p r", r=PACK),
                                        y_sb[:].rearrange("q (p r) -> q p r", r=PACK), rz[:],
-                                       nfs_ps[:].rearrange("q r p -> q p r"), ALU.mult, ALU.mult)
+                                       fs_ps[:].rearrange("q r p -> q p r"), ALU.mult, ALU.mult)
+
         kr1_bf = sb("kr1_bf", [P, T], BF16)
         for h in range(2):
             half = slice(h * T // 2, (h + 1) * T // 2)
@@ -171,35 +178,36 @@ def tile_attend_bresumed_q_kernel(tc, query, keys_words, keys_scales, z0, c00, d
         kr1 = sb("kr1", [P, I], BF16)
         nc.scalar.activation(kr1[:], kr1_bf[:].indirect(offsets[:]), ACT.Copy)
 
-        gt_ps = psum.tile([P, 2, P], F32, name="gt_ps", tag="bank_sz")
+        gt_ps = psum.tile([P, 2, P], F32, name="gt_ps", tag="bank_size")
         gt_bf = sb("gt_bf", [P, Q * PACK], BF16, tag="kr1_bf")
-        turn(gs[:], gt_ps[:], gt_bf[:])
+        turn(neg_gs[:], gt_ps[:], gt_bf[:])
 
-        gather_plane(2, "y_sb")
-        turn_plane(1, kr1)
-        gt_codes = sb("gt_codes", [P, Q], U32)
-        gt_sc = sb("gt_sc", [P, Q], U8)
-        nc.vector.quantize_mx(gt_codes[:].bitcast(FP8X4), gt_sc[:], gt_bf[:])
-        gather_plane(3, "t_sb")
+        turn_window(1, kr1, "kt_ps1")
+        gather_window(3, "y_sb", "kt_ps3")
 
-        kt_codes = sb("kt_codes", [P, D], U32, tag="slot3")
-        kt_sc = sb("kt_sc", [P, D], U8)
+        codes = sb("codes", [P, Q + D], U32, tag="slot3")
+        gt_codes = codes[:, 0:Q]
+        kt_codes = codes[:, Q : Q + D]
+        gt_scales = sb("gt_scales", [P, Q], U8)
+        nc.vector.quantize_mx(gt_codes.bitcast(FP8X4), gt_scales[:], gt_bf[:])
+        kt_scales = sb("kt_scales", [P, D], U8)
 
         def multiply(lo, hi, acc):
-            nc.vector.quantize_mx(kt_codes[:, lo:hi].bitcast(FP8X4), kt_sc[:, lo:hi], kt_bf[:, PACK * lo : PACK * hi])
-            nc.tensor.matmul_mx(acc, lhsT=gt_codes[:].bitcast(FP8X4), lhsT_scale=gt_sc[:],
-                                rhs=kt_codes[:, lo:hi].bitcast(FP8X4), rhs_scale=kt_sc[:, lo:hi],
+            nc.vector.quantize_mx(kt_codes[:, lo:hi].bitcast(FP8X4), kt_scales[:, lo:hi],
+                                  kt_bf[:, PACK * lo : PACK * hi])
+            nc.tensor.matmul_mx(acc, lhsT=gt_codes.bitcast(FP8X4), lhsT_scale=gt_scales[:],
+                                rhs=kt_codes[:, lo:hi].bitcast(FP8X4), rhs_scale=kt_scales[:, lo:hi],
                                 start=True, stop=True)
 
         def finish(lo, hi, acc, tag):
-            y = sb("y%d" % lo, [P, hi - lo], F32, tag=tag)
-            nc.vector.tensor_tensor(y[:], res_sb[:, lo:hi], acc, ALU.subtract)
-            nc.sync.dma_start(out[:, lo:hi], y[:])
+            result = sb("result%d" % lo, [P, hi - lo], F32, tag=tag)
+            nc.vector.tensor_tensor(result[:], res_sb[:, lo:hi], acc, ALU.subtract)
+            nc.sync.dma_start(out[:, lo:hi], result[:])
 
-        acc_a = psum.tile([P, 3 * P], F32, name="acc_a", tag="bank_a")
-        acc_b = psum.tile([P, P], F32, name="acc_b", tag="bank_c")
-        multiply(0, 2 * P, acc_a[:, 0 : 2 * P])
-        multiply(2 * P, 3 * P, acc_a[:, 2 * P : 3 * P])
-        multiply(3 * P, 4 * P, acc_b[:])
-        finish(0, 3 * P, acc_a[:], "kt_bf")
-        finish(3 * P, 4 * P, acc_b[:], "y_last")
+        acc_first = psum.tile([P, 3 * P], F32, name="acc_first", tag="bank_a")
+        acc_last = psum.tile([P, P], F32, name="acc_last", tag="bank_c")
+        multiply(0, 2 * P, acc_first[:, 0 : 2 * P])
+        multiply(2 * P, 3 * P, acc_first[:, 2 * P : 3 * P])
+        multiply(3 * P, 4 * P, acc_last[:])
+        finish(0, 3 * P, acc_first[:], "kt_bf")
+        finish(3 * P, 4 * P, acc_last[:], "result_last")

from contextlib import ExitStack

import concourse.mybir as mybir

D, E, T, I, Q = 512, 512, 2048, 512, 128
FLOPS = 2 * Q * I * (D + E + D)

F32 = mybir.dt.float32
BF16 = mybir.dt.bfloat16
I32 = mybir.dt.int32
U32 = mybir.dt.uint32
U16 = mybir.dt.uint16
U8 = mybir.dt.uint8
FP8X4 = mybir.dt.float8_e4m3fn_x4
FP4X4 = mybir.dt.float4_e2m1fn_x4
ALU = mybir.AluOpType
ACT = mybir.ActivationFunctionType

P = 128
PACK = 4
QUAD = 32
QUADS = P // QUAD
SCALE_ROWS = 16
LAST_QUAD = P - QUAD


def tile_attend_bresumed_q_kernel(tc, query, keys_words, keys_scales, z0, c00, disc, size, gout,
                                   vals_words, vals_scales, fs, keyrows, res, offs, out):
    nc = tc.nc
    with ExitStack() as ctx:
        held = ctx.enter_context(tc.tile_pool(name="held", bufs=1))
        early = ctx.enter_context(tc.tile_pool(name="early", bufs=1))
        psum = ctx.enter_context(tc.psum_pool(name="psum", bufs=1))

        def sb(name, shape, dtype, tag=None):
            return held.tile(shape, dtype, name=name, tag=tag or name, align_bytes=64)

        offsets = held.tile([P, I // 16], U16, name="offsets")
        nc.sync.dma_start(offsets[:], offs)

        ident = sb("ident", [P, P], F32)
        ones = early.tile([P, P], F32, name="ones", offset=0)
        col_no = sb("col_no", [P, P], F32)
        row_no = sb("row_no", [P, QUAD], F32)
        nc.vector.memset(ones[:], 1.0)
        nc.vector.tensor_tensor_scan(col_no[:], ones[:], ones[:], 0.0, ALU.mult, ALU.add)
        nc.vector.transpose(row_no[:], col_no[:, 0:QUAD])
        for a in range(QUADS):
            quad = slice(QUAD * a, QUAD * (a + 1))
            nc.vector.tensor_scalar(ident[quad, :], col_no[quad, :], -float(QUAD * a), row_no[quad, 0:1],
                                    ALU.add, ALU.is_equal)

        ks_win = sb("ks_win", [P, T], U8)
        vs_win = sb("vs_win", [P, T], U8)
        for win, src in ((ks_win, keys_scales), (vs_win, vals_scales)):
            rows = src[0].bitcast(I32).unsqueeze(1).broadcast_to([SCALE_ROWS, QUAD // SCALE_ROWS, T // 4])
            nc.sync.dma_start(win[LAST_QUAD:P, :].bitcast(I32), rows)
            nc.gpsimd.memset(win[0:LAST_QUAD, :].bitcast(I32), 0)

        kw_win = sb("kw_win", [P, T], U16)
        vw_win = sb("vw_win", [P, T], U16)
        q_raw = sb("q_raw", [P, PACK, Q], F32, tag="slot1")
        g_raw = sb("g_raw", [P, PACK, Q], F32, tag="slot2")
        nc.sync.dma_start(kw_win[:].bitcast(I32), keys_words[0].bitcast(I32))
        size_col = sb("size_col", [P, PACK], F32)
        fs_col = sb("fs_col", [P, PACK], F32)
        nc.sync.dma_start(size_col[:], size.rearrange("o (p r) -> (o p) r", r=PACK))
        nc.sync.dma_start(fs_col[:], fs.rearrange("o (p r) -> (o p) r", r=PACK))
        nc.sync.dma_start(q_raw[:], query.rearrange("(p r) q -> p r q", r=PACK))
        nc.sync.dma_start(vw_win[:].bitcast(I32), vals_words[0].bitcast(I32))
        nc.sync.dma_start(g_raw[:], gout.rearrange("(p r) q -> p r q", r=PACK))

        kr_win = []

        def load_window(j):
            kr_win.append(sb("kr_win%d" % j, [P, T], F32, tag="slot%d" % j))
            nc.sync.dma_start(kr_win[j][:], keyrows[P * j : P * (j + 1), :])

        load_window(0)

        z0_col = early.tile([P, 1], F32, name="z0_col", offset=0)
        disc_col = early.tile([P, 1], F32, name="disc_col", offset=64)
        c00_col = early.tile([P, 1], F32, name="c00_col", offset=128)
        kv_scales = sb("kv_scales", [P, 2 * I], U8)
        nc.vector.memset(kv_scales[:].bitcast(I32), 0)
        nc.gpsimd.dma_start(z0_col[:], z0)
        nc.gpsimd.dma_start(disc_col[:], disc)
        nc.gpsimd.dma_start(c00_col[:], c00)

        size_ps = psum.tile([P, PACK, P], F32, name="size_ps", tag="bank_size")
        fs_ps = psum.tile([P, PACK, P], F32, name="fs_ps", tag="bank_fs")
        for r in range(PACK):
            nc.tensor.transpose(size_ps[:, r, :], size_col[:, r : r + 1].to_broadcast([P, P]), ident[:])
        for r in range(PACK):
            nc.tensor.transpose(fs_ps[:, r, :], fs_col[:, r : r + 1].to_broadcast([P, P]), ident[:])
        size_row = sb("size_row", [P, P, PACK], F32)
        nc.scalar.copy(size_row[:], size_ps[:].rearrange("q r p -> q p r"))

        picked = sb("picked", [P, 2 * I], U8)
        nc.vector.tensor_copy(picked[:, 0:I], ks_win[:].indirect(offsets[:]))
        nc.vector.tensor_copy(picked[:, I : 2 * I], vs_win[:].indirect(offsets[:]))
        for a in range(QUADS):
            first = LAST_QUAD + 2 * 4 * a
            nc.sync.dma_start(kv_scales[QUAD * a : QUAD * a + 4, :].bitcast(I32),
                              picked[first : first + 2 * 4 : 2, :].bitcast(I32))

        kw = sb("kw", [P, I], U16)
        vw = sb("vw", [P, I], U16)
        qg_bf = sb("qg_bf", [P, 2, Q, PACK], BF16, tag="slot3")
        qg_codes = sb("qg_codes", [P, 2 * Q], U32, tag="fs_col")
        qg_scales = sb("qg_scales", [P, 2 * Q], U8)
        nc.scalar.activation(qg_bf[:, 0], q_raw[:].rearrange("p r q -> p q r"), ACT.Copy)
        load_window(1)
        nc.vector.tensor_copy(kw[:], kw_win[:].indirect(offsets[:]))
        nc.scalar.copy(qg_bf[:, 1], g_raw[:].rearrange("p r q -> p q r"))
        load_window(2)
        nc.vector.tensor_copy(vw[:], vw_win[:].indirect(offsets[:]))
        nc.vector.quantize_mx(qg_codes[:].bitcast(FP8X4), qg_scales[:], qg_bf[:].rearrange("p s q r -> p (s q r)"))
        load_window(3)

        a_ps = psum.tile([P, I], F32, name="a_ps", tag="bank_a")
        c_ps = psum.tile([P, I], F32, name="c_ps", tag="bank_c")
        nc.tensor.matmul_mx(a_ps[:], lhsT=qg_codes[:, 0:Q].bitcast(FP8X4), lhsT_scale=qg_scales[:, 0:Q],
                            rhs=kw[:].bitcast(FP4X4), rhs_scale=kv_scales[:, 0:I], start=True, stop=True)
        nc.tensor.matmul_mx(c_ps[:], lhsT=qg_codes[:, Q : 2 * Q].bitcast(FP8X4), lhsT_scale=qg_scales[:, Q : 2 * Q],
                            rhs=vw[:].bitcast(FP4X4), rhs_scale=kv_scales[:, I : 2 * I], start=True, stop=True)

        def turn(src_bf, bank, dst_bf):
            words = src_bf.bitcast(F32)
            for u in range(2):
                nc.tensor.transpose(bank[:, u, :], words[:, u : 2 * P : 2], ident[:])
            nc.scalar.copy(dst_bf.bitcast(F32).rearrange("p (x u) -> p x u", u=2), bank.rearrange("p u x -> p x u"))

        kt_bf = sb("kt_bf", [P, D * PACK], BF16)

        def turn_window(j, kr, bank_tag):
            bank = psum.tile([P, 2, P], F32, name="kt_ps%d" % j, tag=bank_tag)
            turn(kr[:], bank[:], kt_bf[:, P * PACK * j : P * PACK * (j + 1)])

        def gather_window(j, tag, bank_tag):
            kr = sb("kr%d" % j, [P, I], BF16, tag=tag)
            nc.vector.tensor_copy(kr[:], kr_win[j][:].indirect(offsets[:]))
            turn_window(j, kr, bank_tag)

        res_sb = sb("res_sb", [P, D], F32, tag="kw")
        nc.sync.dma_start(res_sb[:], res)
        gather_window(0, "kr0", "bank_a")

        p_sb = sb("p_sb", [P, I], F32)
        p_sum = sb("p_sum", [P, 1], F32)
        nc.scalar.activation(p_sb[:], a_ps[:], ACT.Exp, accum_out=p_sum[:])
        z = sb("z", [P, 1], F32)
        nc.scalar.activation(z[:], z0_col[:], ACT.Identity, bias=p_sum[:], scale=disc_col[:])
        cd = early.tile([P, 1], F32, name="cd", offset=0)
        nc.scalar.activation(cd[:], c00_col[:], ACT.Copy, scale=disc_col[:])

        v_sb = sb("v_sb", [P, I], F32, tag="slot0")
        nc.vector.tensor_tensor(v_sb[:], c_ps[:], size_row[:].rearrange("q p r -> q (p r)"), ALU.mult)
        t_sb = sb("t_sb", [P, I], F32)
        t_sum = sb("t_sum", [P, 1], F32)
        nc.vector.scalar_tensor_tensor(t_sb[:], v_sb[:], 1.0, p_sb[:], ALU.mult, ALU.mult, accum_out=t_sum[:])
        rz = sb("rz", [P, 1], F32)
        nc.vector.reciprocal(rz[:], z[:])
        w = sb("w", [P, 1], F32)
        nc.vector.tensor_scalar(w[:], t_sum[:], cd[:], rz[:], ALU.add, ALU.mult)
        y_sb = sb("y_sb", [P, I], F32)
        nc.vector.scalar_tensor_tensor(y_sb[:], p_sb[:], w[:], t_sb[:], ALU.mult, ALU.subtract)
        gather_window(2, "t_sb", "kt_ps2")
        neg_gs = sb("neg_gs", [P, I], BF16, tag="slot2")
        nc.vector.scalar_tensor_tensor(neg_gs[:].rearrange("q (p r) -> q p r", r=PACK),
                                       y_sb[:].rearrange("q (p r) -> q p r", r=PACK), rz[:],
                                       fs_ps[:].rearrange("q r p -> q p r"), ALU.mult, ALU.mult)

        kr1_bf = sb("kr1_bf", [P, T], BF16)
        for h in range(2):
            half = slice(h * T // 2, (h + 1) * T // 2)
            nc.scalar.activation(kr1_bf[:, half], kr_win[1][:, half], ACT.Copy)
        kr1 = sb("kr1", [P, I], BF16)
        nc.scalar.activation(kr1[:], kr1_bf[:].indirect(offsets[:]), ACT.Copy)

        gt_ps = psum.tile([P, 2, P], F32, name="gt_ps", tag="bank_size")
        gt_bf = sb("gt_bf", [P, Q * PACK], BF16, tag="kr1_bf")
        turn(neg_gs[:], gt_ps[:], gt_bf[:])

        turn_window(1, kr1, "kt_ps1")
        gather_window(3, "y_sb", "kt_ps3")

        codes = sb("codes", [P, Q + D], U32, tag="slot3")
        gt_codes = codes[:, 0:Q]
        kt_codes = codes[:, Q : Q + D]
        gt_scales = sb("gt_scales", [P, Q], U8)
        nc.vector.quantize_mx(gt_codes.bitcast(FP8X4), gt_scales[:], gt_bf[:])
        kt_scales = sb("kt_scales", [P, D], U8)

        def multiply(lo, hi, acc):
            nc.vector.quantize_mx(kt_codes[:, lo:hi].bitcast(FP8X4), kt_scales[:, lo:hi],
                                  kt_bf[:, PACK * lo : PACK * hi])
            nc.tensor.matmul_mx(acc, lhsT=gt_codes.bitcast(FP8X4), lhsT_scale=gt_scales[:],
                                rhs=kt_codes[:, lo:hi].bitcast(FP8X4), rhs_scale=kt_scales[:, lo:hi],
                                start=True, stop=True)

        def finish(lo, hi, acc, tag):
            result = sb("result%d" % lo, [P, hi - lo], F32, tag=tag)
            nc.vector.tensor_tensor(result[:], res_sb[:, lo:hi], acc, ALU.subtract)
            nc.sync.dma_start(out[:, lo:hi], result[:])

        acc_first = psum.tile([P, 3 * P], F32, name="acc_first", tag="bank_a")
        acc_last = psum.tile([P, P], F32, name="acc_last", tag="bank_c")
        multiply(0, 2 * P, acc_first[:, 0 : 2 * P])
        multiply(2 * P, 3 * P, acc_first[:, 2 * P : 3 * P])
        multiply(3 * P, 4 * P, acc_last[:])
        finish(0, 3 * P, acc_first[:], "kt_bf")
        finish(3 * P, 4 * P, acc_last[:], "result_last")
